import numpy as np
import ml_dtypes


def mxq(x, axis, fmt="e4m3"):
    dtype, down = {"e4m3": (ml_dtypes.float8_e4m3fn, 7), "e5m2": (ml_dtypes.float8_e5m2, 14)}[fmt]
    v = np.moveaxis(np.asarray(x, np.float32).astype(ml_dtypes.bfloat16).astype(np.float64), axis, -1)
    blocks = v.reshape(v.shape[:-1] + (-1, 32))
    amax = np.abs(blocks).max(-1, keepdims=True)
    byte = np.maximum(np.where(amax > 0, np.frexp(amax)[1] - 1 + 127, 0) - down, 1)
    scale = np.exp2(byte - 127.0)
    codes = (blocks / scale).astype(np.float32).astype(dtype).astype(np.float64)
    return np.moveaxis((codes * scale).reshape(v.shape), -1, axis)


WIDE = False


def mx_kscale(k):
    if not WIDE:
        return np.ones(k)
    levels = np.array([10, -10, 5, -5, 0])
    if k % 512:
        return np.exp2(np.random.permutation(np.resize(levels, k // 32))).repeat(32)
    a = np.empty((k // 512, 16))
    for p in range(k // 512):
        a[p, :8] = np.random.permutation(np.resize(levels, 8))
        for g in range(8):
            far = levels[np.abs(levels - a[p, g]) >= 10]
            a[p, g + 8] = far[np.random.randint(len(far))]
    return np.exp2(a.ravel()).repeat(32)


def f64(x):
    return np.asarray(x).astype(np.float64)


def striped8(idx):
    return np.concatenate([v.reshape(-1, 16).T for v in idx]).astype(np.uint16)


def unstriped8(offs):
    return np.stack([offs[16 * g:16 * g + 16].T.reshape(-1) for g in range(8)]).astype(np.int64)


def split(x):
    m, e = np.frexp(f64(x))
    hi = np.ldexp(np.trunc(16.0 * m) / 16.0, e)
    return hi, f64(x) - hi


K, M, T, S = 2048, 256, 2048, 512


def setup_inputs():
    n = np.random.standard_normal
    s = mx_kscale(K)[:, None]
    return {
        "xT": (n((K, T)) * s).astype(np.float32),
        "w": (n((K, M)) / np.sqrt(K) / s).astype(np.float32),
        "wgt": np.repeat(np.random.uniform(0.5, 2.0, (8, S)), 16, axis=0).astype(np.float32),
        "offs": striped8(np.stack([np.random.permutation(T)[:S] for _ in range(8)])),
    }


def reference(xT, w, wgt, offs):
    idx = unstriped8(offs)
    group = np.arange(K) % 512 // 64
    xg = f64(wgt)[np.arange(K) // 4 % 128] * f64(xT)[np.arange(K)[:, None], idx[group]]
    xT_ = mxq(xg, 0, "e4m3")
    w_hi, w_lo = split(w)
    w_hi_, w_lo_ = mxq(w_hi, 0, "e4m3"), mxq(w_lo, 0, "e4m3")
    y = xT_.T @ w_hi_ + xT_.T @ w_lo_
    return y

@@ -1,0 +1,140 @@
+from contextlib import ExitStack
+
+import concourse.mybir as mybir
+
+K, M, T, S = 2048, 256, 2048, 512
+FLOPS = 2 * 2 * K * M * S
+
+F32 = mybir.dt.float32
+BF16 = mybir.dt.bfloat16
+I32 = mybir.dt.int32
+U32 = mybir.dt.uint32
+U16 = mybir.dt.uint16
+U8 = mybir.dt.uint8
+FP8X4 = mybir.dt.float8_e4m3fn_x4
+MULT = mybir.AluOpType.mult
+SUB = mybir.AluOpType.subtract
+AND = mybir.AluOpType.bitwise_and
+
+P = 128
+PACK = 4
+K_PASS = P * PACK
+PASSES = K // K_PASS
+J_TILE = 128
+HI_MASK = -0x000F0010
+
+
+def tile_list_heads_tm_hl_none_kernel(tc, xT, w, wgt, offs, out):
+    nc = tc.nc
+    with ExitStack() as ctx:
+        lists = ctx.enter_context(tc.tile_pool(name="lists", bufs=1))
+        keep = ctx.enter_context(tc.tile_pool(name="keep", bufs=1))
+        work = ctx.enter_context(tc.tile_pool(name="work", bufs=2))
+        psum = ctx.enter_context(tc.psum_pool(name="psum", bufs=1))
+
+        offs_sb = lists.tile([P, S // 16], U16, name="offs_sb")
+        nc.sync.dma_start(offs_sb[:], offs)
+
+        planes = [[keep.tile([P, T], F32, name=f"x_{a}_{i}") for i in range(PACK)] for a in range(PASSES)]
+        w_f32 = [keep.tile([P, PACK, M], F32, name=f"w_{a}") for a in range(PASSES)]
+        wgt_sb = keep.tile([P, S], F32, name="wgt_sb")
+
+        def load_w(a):
+            nc.sync.dma_start(w_f32[a][:], w[a * K_PASS : (a + 1) * K_PASS, :].rearrange("(p i) n -> p i n", i=PACK))
+
+        def load_plane(a, i):
+            rows = xT[a * K_PASS : (a + 1) * K_PASS, :].rearrange("(p i) t -> p i t", i=PACK)
+            nc.sync.dma_start(planes[a][i][:], rows[:, i, :])
+
+        load_w(0)
+        nc.sync.dma_start(wgt_sb[:], wgt)
+        load_plane(0, 0)
+        load_w(1)
+        load_plane(0, 1)
+        load_w(2)
+        load_plane(0, 2)
+        load_w(3)
+        load_plane(0, 3)
+        for a in range(1, PASSES):
+            for i in range(PACK):
+                load_plane(a, i)
+
+        x_codes = [keep.tile([P, S], U32, name=f"xc_{a}", align_bytes=64) for a in range(PASSES)]
+        x_scales = [keep.tile([P, S], U8, name=f"xs_{a}", align_bytes=64) for a in range(PASSES)]
+        hi_codes = [keep.tile([P, M], U32, name=f"hc_{a}", align_bytes=64) for a in range(PASSES)]
+        hi_scales = [keep.tile([P, M], U8, name=f"hs_{a}", align_bytes=64) for a in range(PASSES)]
+        lo_codes = [keep.tile([P, M], U32, name=f"lc_{a}", align_bytes=64) for a in range(PASSES)]
+        lo_scales = [keep.tile([P, M], U8, name=f"ls_{a}", align_bytes=64) for a in range(PASSES)]
+        sums = [psum.tile([J_TILE, M], F32, name=f"sum_{j}") for j in range(S // J_TILE)]
+
+        def interleaved(tile):
+            return tile[:].rearrange("p (c m i) -> p c i m", m=4, i=PACK)
+
+        def split_w(a):
+            raw = work.tile([P, M * PACK], BF16, name="w_raw", align_bytes=64)
+            hi = work.tile([P, M * PACK], BF16, name="w_hi", align_bytes=64)
+            lo = work.tile([P, M * PACK], BF16, name="w_lo", align_bytes=64)
+            halves = w_f32[a][:].bitcast(BF16).rearrange("p i (c m h) -> p c i m h", m=4, h=2)
+            nc.scalar.copy(interleaved(raw), halves[:, :, :, :, 1])
+            nc.vector.tensor_scalar(hi[:].bitcast(I32), raw[:].bitcast(I32), HI_MASK, None, AND)
+            nc.vector.tensor_tensor(
+                interleaved(lo), w_f32[a][:].rearrange("p i (c m) -> p c i m", m=4), interleaved(hi), SUB
+            )
+            nc.vector.quantize_mx(out=hi_codes[a][:].bitcast(FP8X4), scales=hi_scales[a][:], in_=hi[:])
+            nc.vector.quantize_mx(out=lo_codes[a][:].bitcast(FP8X4), scales=lo_scales[a][:], in_=lo[:])
+
+        def pick(a, i, j0, width, picked):
+            nc.vector.tensor_tensor(
+                picked[:, i, :],
+                planes[a][i][:].indirect(offs_sb[:, j0 // 16 : (j0 + width) // 16]),
+                wgt_sb[:, j0 : j0 + width],
+                MULT,
+            )
+
+        def round_and_quantise(a, j0, width, picked, engine):
+            rounded = work.tile([P, width * PACK], BF16, name=f"rounded_{width}", align_bytes=64)
+            source = picked[:].rearrange("p i (c m) -> p c i m", m=4)
+            if engine == "scalar":
+                nc.scalar.copy(interleaved(rounded), source)
+            else:
+                nc.vector.tensor_copy(interleaved(rounded), source)
+            nc.vector.quantize_mx(
+                out=x_codes[a][:, j0 : j0 + width].bitcast(FP8X4), scales=x_scales[a][:, j0 : j0 + width], in_=rounded[:]
+            )
+
+        def multiply(a, j):
+            cols = slice(j * J_TILE, (j + 1) * J_TILE)
+            for codes, scales, last in ((hi_codes[a], hi_scales[a], False), (lo_codes[a], lo_scales[a], True)):
+                nc.tensor.matmul_mx(
+                    out=sums[j][:],
+                    lhsT=x_codes[a][:, cols].bitcast(FP8X4),
+                    lhsT_scale=x_scales[a][:, cols],
+                    rhs=codes[:].bitcast(FP8X4),
+                    rhs_scale=scales[:],
+                    start=(a == 0 and not last),
+                    stop=(a == PASSES - 1 and last),
+                )
+
+        split_w(0)
+        for a in range(PASSES):
+            width = 256 if a < PASSES - 1 else J_TILE
+            starts = range(0, S, width)
+            picked = [work.tile([P, PACK, width], F32, name=f"picked_{width}_{j0}") for j0 in starts]
+            for i in range(PACK):
+                for s, j0 in enumerate(starts):
+                    pick(a, i, j0, width, picked[s])
+                if a == 0 and i < PASSES - 1:
+                    split_w(i + 1)
+            for s, j0 in enumerate(starts):
+                on_vector = a == PASSES - 1 and s == 3
+                round_and_quantise(a, j0, width, picked[s], "vector" if on_vector else "scalar")
+                for j in range(j0 // J_TILE, (j0 + width) // J_TILE):
+                    multiply(a, j)
+
+        for j in range(S // J_TILE):
+            result = keep.tile([J_TILE, M], F32, name=f"result_{j}")
+            if j < 3:
+                nc.scalar.copy(result[:], sums[j][:])
+            else:
+                nc.vector.tensor_copy(result[:], sums[j][:])
+            nc.sync.dma_start(out[j * J_TILE : (j + 1) * J_TILE, :], result[:])

@@ -21,7 +21,7 @@ PACK = 4
 K_PASS = P * PACK
 PASSES = K // K_PASS
 J_TILE = 128
-HI_MASK = -0x000F0010
+HI_MASK = -0x00100000
 
 
 def tile_list_heads_tm_hl_none_kernel(tc, xT, w, wgt, offs, out):
@@ -48,93 +48,115 @@ def tile_list_heads_tm_hl_none_kernel(tc, xT, w, wgt, offs, out):
 
         load_w(0)
         nc.sync.dma_start(wgt_sb[:], wgt)
-        load_plane(0, 0)
         load_w(1)
-        load_plane(0, 1)
+        load_plane(0, 0)
         load_w(2)
-        load_plane(0, 2)
         load_w(3)
-        load_plane(0, 3)
-        for a in range(1, PASSES):
+        for a in range(PASSES):
             for i in range(PACK):
-                load_plane(a, i)
+                if (a, i) != (0, 0):
+                    load_plane(a, i)
 
         x_codes = [keep.tile([P, S], U32, name=f"xc_{a}", align_bytes=64) for a in range(PASSES)]
         x_scales = [keep.tile([P, S], U8, name=f"xs_{a}", align_bytes=64) for a in range(PASSES)]
-        hi_codes = [keep.tile([P, M], U32, name=f"hc_{a}", align_bytes=64) for a in range(PASSES)]
-        hi_scales = [keep.tile([P, M], U8, name=f"hs_{a}", align_bytes=64) for a in range(PASSES)]
-        lo_codes = [keep.tile([P, M], U32, name=f"lc_{a}", align_bytes=64) for a in range(PASSES)]
-        lo_scales = [keep.tile([P, M], U8, name=f"ls_{a}", align_bytes=64) for a in range(PASSES)]
-        sums = [psum.tile([J_TILE, M], F32, name=f"sum_{j}") for j in range(S // J_TILE)]
+        w_codes = [keep.tile([P, 2 * M], U32, name=f"wc_{a}", align_bytes=64) for a in range(PASSES)]
+        w_scales = [keep.tile([P, 2 * M], U8, name=f"ws_{a}", align_bytes=64) for a in range(PASSES)]
+        sums = [[(slice(0, M), psum.tile([J_TILE, M], F32, name=f"sum_{j}"))] for j in range(3)]
+        sums.append([(slice(h, h + 128), psum.tile([J_TILE, 128], F32, name=f"sum_3_{h}")) for h in (0, 128)])
 
-        def interleaved(tile):
-            return tile[:].rearrange("p (c m i) -> p c i m", m=4, i=PACK)
+        def round_to(columns, planes_f32):
+            nc.scalar.copy(
+                columns.rearrange("p (c m) i -> p c i m", m=4), planes_f32.rearrange("p i (c m) -> p c i m", m=4)
+            )
 
         def split_w(a):
-            raw = work.tile([P, M * PACK], BF16, name="w_raw", align_bytes=64)
-            hi = work.tile([P, M * PACK], BF16, name="w_hi", align_bytes=64)
-            lo = work.tile([P, M * PACK], BF16, name="w_lo", align_bytes=64)
-            halves = w_f32[a][:].bitcast(BF16).rearrange("p i (c m h) -> p c i m h", m=4, h=2)
-            nc.scalar.copy(interleaved(raw), halves[:, :, :, :, 1])
-            nc.vector.tensor_scalar(hi[:].bitcast(I32), raw[:].bitcast(I32), HI_MASK, None, AND)
-            nc.vector.tensor_tensor(
-                interleaved(lo), w_f32[a][:].rearrange("p i (c m) -> p c i m", m=4), interleaved(hi), SUB
+            hi = work.tile([P, PACK, M], F32, name="w_hi")
+            lo = work.tile([P, PACK, M], F32, name="w_lo")
+            rounded = work.tile([P, 2 * M, PACK], BF16, name="w_rounded", align_bytes=64)
+            nc.vector.tensor_scalar(hi[:].bitcast(I32), w_f32[a][:].bitcast(I32), HI_MASK, None, AND)
+            nc.vector.tensor_tensor(lo[:], w_f32[a][:], hi[:], SUB)
+            round_to(rounded[:, :M, :], hi[:])
+            round_to(rounded[:, M:, :], lo[:])
+            return rounded
+
+        def quantise_w(a, rounded):
+            nc.vector.quantize_mx(
+                out=w_codes[a][:].bitcast(FP8X4), scales=w_scales[a][:], in_=rounded[:].rearrange("p n i -> p (n i)")
             )
-            nc.vector.quantize_mx(out=hi_codes[a][:].bitcast(FP8X4), scales=hi_scales[a][:], in_=hi[:])
-            nc.vector.quantize_mx(out=lo_codes[a][:].bitcast(FP8X4), scales=lo_scales[a][:], in_=lo[:])
 
         def pick(a, i, j0, width, picked):
             nc.vector.tensor_tensor(
-                picked[:, i, :],
+                picked,
                 planes[a][i][:].indirect(offs_sb[:, j0 // 16 : (j0 + width) // 16]),
                 wgt_sb[:, j0 : j0 + width],
                 MULT,
             )
 
-        def round_and_quantise(a, j0, width, picked, engine):
-            rounded = work.tile([P, width * PACK], BF16, name=f"rounded_{width}", align_bytes=64)
-            source = picked[:].rearrange("p i (c m) -> p c i m", m=4)
-            if engine == "scalar":
-                nc.scalar.copy(interleaved(rounded), source)
-            else:
-                nc.vector.tensor_copy(interleaved(rounded), source)
+        def quantise(a, j0, width, rounded):
             nc.vector.quantize_mx(
-                out=x_codes[a][:, j0 : j0 + width].bitcast(FP8X4), scales=x_scales[a][:, j0 : j0 + width], in_=rounded[:]
+                out=x_codes[a][:, j0 : j0 + width].bitcast(FP8X4), scales=x_scales[a][:, j0 : j0 + width], in_=rounded
             )
 
         def multiply(a, j):
             cols = slice(j * J_TILE, (j + 1) * J_TILE)
-            for codes, scales, last in ((hi_codes[a], hi_scales[a], False), (lo_codes[a], lo_scales[a], True)):
-                nc.tensor.matmul_mx(
-                    out=sums[j][:],
-                    lhsT=x_codes[a][:, cols].bitcast(FP8X4),
-                    lhsT_scale=x_scales[a][:, cols],
-                    rhs=codes[:].bitcast(FP8X4),
-                    rhs_scale=scales[:],
-                    start=(a == 0 and not last),
-                    stop=(a == PASSES - 1 and last),
-                )
+            for n_cols, total in sums[j]:
+                for part in range(2):
+                    w_cols = slice(part * M + n_cols.start, part * M + n_cols.stop)
+                    nc.tensor.matmul_mx(
+                        out=total[:],
+                        lhsT=x_codes[a][:, cols].bitcast(FP8X4),
+                        lhsT_scale=x_scales[a][:, cols],
+                        rhs=w_codes[a][:, w_cols].bitcast(FP8X4),
+                        rhs_scale=w_scales[a][:, w_cols],
+                        start=(a == 0 and part == 0),
+                        stop=(a == PASSES - 1 and part == 1),
+                    )
 
-        split_w(0)
-        for a in range(PASSES):
-            width = 256 if a < PASSES - 1 else J_TILE
-            starts = range(0, S, width)
-            picked = [work.tile([P, PACK, width], F32, name=f"picked_{width}_{j0}") for j0 in starts]
+        def finish(a, rounded):
+            quantise(a, 0, S, rounded[:].rearrange("p j i -> p (j i)"))
+            for j in range(S // J_TILE):
+                multiply(a, j)
+
+        w_rounded = [split_w(0), split_w(1)]
+        waiting = None
+        for a in range(PASSES - 1):
+            picked = work.tile([P, PACK, S], F32, name="picked")
             for i in range(PACK):
-                for s, j0 in enumerate(starts):
-                    pick(a, i, j0, width, picked[s])
-                if a == 0 and i < PASSES - 1:
-                    split_w(i + 1)
-            for s, j0 in enumerate(starts):
-                on_vector = a == PASSES - 1 and s == 3
-                round_and_quantise(a, j0, width, picked[s], "vector" if on_vector else "scalar")
-                for j in range(j0 // J_TILE, (j0 + width) // J_TILE):
-                    multiply(a, j)
+                for j0 in (0, 256):
+                    pick(a, i, j0, 256, picked[:, i, j0 : j0 + 256])
+                if a == 0 and i == 0:
+                    for b in range(2):
+                        quantise_w(b, w_rounded[b])
+                    w_rounded = [split_w(2), split_w(3)]
+                if a == 0 and i == 1:
+                    for b in range(2):
+                        quantise_w(b + 2, w_rounded[b])
+                if a > 0 and i == 1:
+                    finish(a - 1, waiting)
+            waiting = work.tile([P, S, PACK], BF16, name="rounded", align_bytes=64)
+            for j0 in (0, 256):
+                round_to(waiting[:, j0 : j0 + 256, :], picked[:, :, j0 : j0 + 256])
+
+        a = PASSES - 1
+        rounded_last = keep.tile([P, S, PACK], BF16, name="rounded_last", align_bytes=64)
+        for i in range(PACK):
+            width = 256 if i < PACK - 1 else J_TILE
+            picked_last = keep.tile([P, S], F32, name=f"picked_last_{i}")
+            for j0 in range(0, S, width):
+                pick(a, i, j0, width, picked_last[:, j0 : j0 + width])
+                nc.scalar.copy(rounded_last[:, j0 : j0 + width, i], picked_last[:, j0 : j0 + width])
+            if i == 2:
+                finish(a - 1, waiting)
+        for j in range(S // J_TILE):
+            j0 = j * J_TILE
+            quantise(a, j0, J_TILE, rounded_last[:, j0 : j0 + J_TILE, :].rearrange("p j i -> p (j i)"))
+            multiply(a, j)
 
         for j in range(S // J_TILE):
             result = keep.tile([J_TILE, M], F32, name=f"result_{j}")
-            if j < 3:
-                nc.scalar.copy(result[:], sums[j][:])
-            else:
-                nc.vector.tensor_copy(result[:], sums[j][:])
+            for n_cols, total in sums[j]:
+                if j == 1 or (j == 3 and n_cols.start == 0):
+                    nc.vector.tensor_copy(result[:, n_cols], total[:])
+                else:
+                    nc.scalar.copy(result[:, n_cols], total[:])
             nc.sync.dma_start(out[j * J_TILE : (j + 1) * J_TILE, :], result[:])

from contextlib import ExitStack

import concourse.mybir as mybir

K, M, T, S = 2048, 256, 2048, 512
FLOPS = 2 * 2 * K * M * S

F32 = mybir.dt.float32
BF16 = mybir.dt.bfloat16
I32 = mybir.dt.int32
U32 = mybir.dt.uint32
U16 = mybir.dt.uint16
U8 = mybir.dt.uint8
FP8X4 = mybir.dt.float8_e4m3fn_x4
MULT = mybir.AluOpType.mult
SUB = mybir.AluOpType.subtract
AND = mybir.AluOpType.bitwise_and

P = 128
PACK = 4
K_PASS = P * PACK
PASSES = K // K_PASS
J_TILE = 128
HI_MASK = -0x00100000


def tile_list_heads_tm_hl_none_kernel(tc, xT, w, wgt, offs, out):
    nc = tc.nc
    with ExitStack() as ctx:
        lists = ctx.enter_context(tc.tile_pool(name="lists", bufs=1))
        keep = ctx.enter_context(tc.tile_pool(name="keep", bufs=1))
        work = ctx.enter_context(tc.tile_pool(name="work", bufs=2))
        psum = ctx.enter_context(tc.psum_pool(name="psum", bufs=1))

        offs_sb = lists.tile([P, S // 16], U16, name="offs_sb")
        nc.sync.dma_start(offs_sb[:], offs)

        planes = [[keep.tile([P, T], F32, name=f"x_{a}_{i}") for i in range(PACK)] for a in range(PASSES)]
        w_f32 = [keep.tile([P, PACK, M], F32, name=f"w_{a}") for a in range(PASSES)]
        wgt_sb = keep.tile([P, S], F32, name="wgt_sb")

        def load_w(a):
            nc.sync.dma_start(w_f32[a][:], w[a * K_PASS : (a + 1) * K_PASS, :].rearrange("(p i) n -> p i n", i=PACK))

        def load_plane(a, i):
            rows = xT[a * K_PASS : (a + 1) * K_PASS, :].rearrange("(p i) t -> p i t", i=PACK)
            nc.sync.dma_start(planes[a][i][:], rows[:, i, :])

        load_w(0)
        nc.sync.dma_start(wgt_sb[:], wgt)
        load_w(1)
        load_plane(0, 0)
        load_w(2)
        load_w(3)
        for a in range(PASSES):
            for i in range(PACK):
                if (a, i) != (0, 0):
                    load_plane(a, i)

        x_codes = [keep.tile([P, S], U32, name=f"xc_{a}", align_bytes=64) for a in range(PASSES)]
        x_scales = [keep.tile([P, S], U8, name=f"xs_{a}", align_bytes=64) for a in range(PASSES)]
        w_codes = [keep.tile([P, 2 * M], U32, name=f"wc_{a}", align_bytes=64) for a in range(PASSES)]
        w_scales = [keep.tile([P, 2 * M], U8, name=f"ws_{a}", align_bytes=64) for a in range(PASSES)]
        sums = [[(slice(0, M), psum.tile([J_TILE, M], F32, name=f"sum_{j}"))] for j in range(3)]
        sums.append([(slice(h, h + 128), psum.tile([J_TILE, 128], F32, name=f"sum_3_{h}")) for h in (0, 128)])

        def round_to(columns, planes_f32):
            nc.scalar.copy(
                columns.rearrange("p (c m) i -> p c i m", m=4), planes_f32.rearrange("p i (c m) -> p c i m", m=4)
            )

        def split_w(a):
            hi = work.tile([P, PACK, M], F32, name="w_hi")
            lo = work.tile([P, PACK, M], F32, name="w_lo")
            rounded = work.tile([P, 2 * M, PACK], BF16, name="w_rounded", align_bytes=64)
            nc.vector.tensor_scalar(hi[:].bitcast(I32), w_f32[a][:].bitcast(I32), HI_MASK, None, AND)
            nc.vector.tensor_tensor(lo[:], w_f32[a][:], hi[:], SUB)
            round_to(rounded[:, :M, :], hi[:])
            round_to(rounded[:, M:, :], lo[:])
            return rounded

        def quantise_w(a, rounded):
            nc.vector.quantize_mx(
                out=w_codes[a][:].bitcast(FP8X4), scales=w_scales[a][:], in_=rounded[:].rearrange("p n i -> p (n i)")
            )

        def pick(a, i, j0, width, picked):
            nc.vector.tensor_tensor(
                picked,
                planes[a][i][:].indirect(offs_sb[:, j0 // 16 : (j0 + width) // 16]),
                wgt_sb[:, j0 : j0 + width],
                MULT,
            )

        def quantise(a, j0, width, rounded):
            nc.vector.quantize_mx(
                out=x_codes[a][:, j0 : j0 + width].bitcast(FP8X4), scales=x_scales[a][:, j0 : j0 + width], in_=rounded
            )

        def multiply(a, j):
            cols = slice(j * J_TILE, (j + 1) * J_TILE)
            for n_cols, total in sums[j]:
                for part in range(2):
                    w_cols = slice(part * M + n_cols.start, part * M + n_cols.stop)
                    nc.tensor.matmul_mx(
                        out=total[:],
                        lhsT=x_codes[a][:, cols].bitcast(FP8X4),
                        lhsT_scale=x_scales[a][:, cols],
                        rhs=w_codes[a][:, w_cols].bitcast(FP8X4),
                        rhs_scale=w_scales[a][:, w_cols],
                        start=(a == 0 and part == 0),
                        stop=(a == PASSES - 1 and part == 1),
                    )

        def finish(a, rounded):
            quantise(a, 0, S, rounded[:].rearrange("p j i -> p (j i)"))
            for j in range(S // J_TILE):
                multiply(a, j)

        w_rounded = [split_w(0), split_w(1)]
        waiting = None
        for a in range(PASSES - 1):
            picked = work.tile([P, PACK, S], F32, name="picked")
            for i in range(PACK):
                for j0 in (0, 256):
                    pick(a, i, j0, 256, picked[:, i, j0 : j0 + 256])
                if a == 0 and i == 0:
                    for b in range(2):
                        quantise_w(b, w_rounded[b])
                    w_rounded = [split_w(2), split_w(3)]
                if a == 0 and i == 1:
                    for b in range(2):
                        quantise_w(b + 2, w_rounded[b])
                if a > 0 and i == 1:
                    finish(a - 1, waiting)
            waiting = work.tile([P, S, PACK], BF16, name="rounded", align_bytes=64)
            for j0 in (0, 256):
                round_to(waiting[:, j0 : j0 + 256, :], picked[:, :, j0 : j0 + 256])

        a = PASSES - 1
        rounded_last = keep.tile([P, S, PACK], BF16, name="rounded_last", align_bytes=64)
        for i in range(PACK):
            width = 256 if i < PACK - 1 else J_TILE
            picked_last = keep.tile([P, S], F32, name=f"picked_last_{i}")
            for j0 in range(0, S, width):
                pick(a, i, j0, width, picked_last[:, j0 : j0 + width])
                nc.scalar.copy(rounded_last[:, j0 : j0 + width, i], picked_last[:, j0 : j0 + width])
            if i == 2:
                finish(a - 1, waiting)
        for j in range(S // J_TILE):
            j0 = j * J_TILE
            quantise(a, j0, J_TILE, rounded_last[:, j0 : j0 + J_TILE, :].rearrange("p j i -> p (j i)"))
            multiply(a, j)

        for j in range(S // J_TILE):
            result = keep.tile([J_TILE, M], F32, name=f"result_{j}")
            for n_cols, total in sums[j]:
                if j == 1 or (j == 3 and n_cols.start == 0):
                    nc.vector.tensor_copy(result[:, n_cols], total[:])
                else:
                    nc.scalar.copy(result[:, n_cols], total[:])
            nc.sync.dma_start(out[j * J_TILE : (j + 1) * J_TILE, :], result[:])
